import numpy as np
import ml_dtypes


def mxq(x, axis, fmt="e4m3"):
    dtype, down = {"e4m3": (ml_dtypes.float8_e4m3fn, 7), "e5m2": (ml_dtypes.float8_e5m2, 14)}[fmt]
    v = np.moveaxis(np.asarray(x, np.float32).astype(ml_dtypes.bfloat16).astype(np.float64), axis, -1)
    blocks = v.reshape(v.shape[:-1] + (-1, 32))
    amax = np.abs(blocks).max(-1, keepdims=True)
    byte = np.maximum(np.where(amax > 0, np.frexp(amax)[1] - 1 + 127, 0) - down, 1)
    scale = np.exp2(byte - 127.0)
    codes = (blocks / scale).astype(np.float32).astype(dtype).astype(np.float64)
    return np.moveaxis((codes * scale).reshape(v.shape), -1, axis)


WIDE = False


def mx_kscale(k):
    if not WIDE:
        return np.ones(k)
    levels = np.array([10, -10, 5, -5, 0])
    if k % 512:
        return np.exp2(np.random.permutation(np.resize(levels, k // 32))).repeat(32)
    a = np.empty((k // 512, 16))
    for p in range(k // 512):
        a[p, :8] = np.random.permutation(np.resize(levels, 8))
        for g in range(8):
            far = levels[np.abs(levels - a[p, g]) >= 10]
            a[p, g + 8] = far[np.random.randint(len(far))]
    return np.exp2(a.ravel()).repeat(32)


def f64(x):
    return np.asarray(x).astype(np.float64)


def striped(idx):
    return np.tile(idx.reshape(-1, 16).T, (8, 1)).astype(np.uint16)


def unstriped(offs):
    return offs[:16].T.reshape(-1).astype(np.int64)


def gelu(v):
    return 0.5 * v * (1.0 + np.tanh(np.sqrt(2.0 / np.pi) * (v + 0.044715 * v**3)))


K, T, S, H, N = 512, 4096, 1536, 512, 256


def setup_inputs():
    n = np.random.standard_normal
    s = mx_kscale(K)[:, None]
    u = mx_kscale(H)
    return {
        "xT": (n((K, T)) * s).astype(np.float32),
        "w1": (n((K, H)) / np.sqrt(K) / s).astype(np.float32),
        "w3": (n((K, H)) / np.sqrt(K) / s * u).astype(np.float32),
        "w2": (n((H, N)) / np.sqrt(H) / u[:, None]).astype(np.float32),
        "offs": striped(np.sort(np.random.permutation(T)[:S])),
    }


def reference(xT, w1, w3, w2, offs):
    idx = unstriped(offs)
    xq = mxq(f64(xT)[:, idx], 0, "e4m3")
    h = gelu(mxq(f64(w1), 0, "e4m3").T @ xq) * (mxq(f64(w3), 0, "e4m3").T @ xq)
    y = mxq(f64(w2), 0, "e4m3").T @ mxq(h, 0, "e4m3")
    return y

from contextlib import ExitStack

import concourse.mybir as mybir

K, T, S, H, N = 512, 4096, 1536, 512, 256
FLOPS = 2 * S * (2 * K * H + H * N)

F32 = mybir.dt.float32
BF16 = mybir.dt.bfloat16
U32 = mybir.dt.uint32
I32 = mybir.dt.int32
U16 = mybir.dt.uint16
U8 = mybir.dt.uint8
FP8X4 = mybir.dt.float8_e4m3fn_x4
GELU = mybir.ActivationFunctionType.Gelu_apprx_tanh
MULT = mybir.AluOpType.mult
ADD = mybir.AluOpType.add

P = 128
PACK = 4
SUB = 128
CHUNKS = ((512,"v",),(512,"s",),(512,"v",),(512,"s",),(512,"v",),(256,"s",),(128,"v",),(256,"s",),(256,"s",),(256,"s",),(256,"s",),(128,"v",),)
SLICES = ((0,384,),(384,896,),(896,1536,),)
TEXT = ("x0","x1","x2","x3","x4","x5","x6","g0","x7","x8","w1","u0","g1","x9","x10","x11","w3","w2","r0","g2","u1","r1","u2","r2",)
LOADS = ("x0","offs","x1","x2","x3","x4","x5","x6","x7","x8","w1","x9","x10","x11","w3","w2",)
W_ENGINES = {"w1": "sg", "w3": "gs", "w2": "g"}
Y_ENGINES = "s" * 12


def tile_picked_pick_glu_gelu_srt_e_kernel(tc, xT, w1, w3, w2, offs, out):
    nc = tc.nc

    def copy(engine, dst, src):
        if engine == "v":
            nc.vector.tensor_copy(dst, src)
        elif engine == "s":
            nc.scalar.copy(dst, src)
        else:
            nc.gpsimd.tensor_scalar(dst, src, 1.0, 0.0, MULT, ADD)

    with ExitStack() as ctx:
        keep = ctx.enter_context(tc.tile_pool(name="keep", bufs=1))
        hidden = ctx.enter_context(tc.tile_pool(name="hidden", bufs=3))
        gates = ctx.enter_context(tc.tile_pool(name="gates", bufs=12))
        psum = ctx.enter_context(tc.psum_pool(name="psum", bufs=3))
        psum_y = ctx.enter_context(tc.psum_pool(name="psum_y", bufs=2))

        offsets = keep.tile([P, S // 16], U16, name="offsets")
        warm = keep.tile([P, 2], F32, name="warm")
        codes = keep.tile([P, T], U32, name="codes", align_bytes=64)
        planes = keep.tile([P, T], U8, name="planes", align_bytes=64)
        wt = {}
        for name, src, cols in (("w1", w1, H), ("w3", w3, H), ("w2", w2, N)):
            raw = keep.tile([P, PACK, cols], F32, name=name + "_raw")
            bf = keep.tile([P, cols * PACK], BF16, name=name + "_bf", align_bytes=64)
            wc = keep.tile([P, cols], U32, name=name + "_codes", align_bytes=64)
            ws = keep.tile([P, cols], U8, name=name + "_planes", align_bytes=64)
            wt[name] = (raw, bf, wc, ws, src.rearrange("(p j) c -> p j c", j=PACK))

        tokens = xT.rearrange("(p j) t -> p j t", j=PACK)
        raws = []
        starts = []
        at = 0
        for c, (size, engine) in enumerate(CHUNKS):
            raw = keep.tile([P, PACK, size], F32, name="raw%d" % c)
            raws.append(raw)
            starts.append(at)
            at += size

        nc.vector.memset(warm[:], 0.0)
        nc.scalar.activation(warm[:, 1:2], warm[:, 0:1], GELU)
        nc.gpsimd.memset(planes[:].bitcast(I32), 0)

        for item in LOADS:
            if item == "offs":
                nc.sync.dma_start(offsets[:], offs)
            elif item in wt:
                nc.sync.dma_start(wt[item][0][:], wt[item][4])
            else:
                c = int(item[1:])
                nc.sync.dma_start(raws[c][:], tokens[:, :, starts[c] : starts[c] + CHUNKS[c][0]])

        picked = {}
        gelus = {}

        def chunk(c):
            size, engine = CHUNKS[c]
            g = keep.tile([P, size, PACK], BF16, name="grouped%d" % c, align_bytes=64)
            copy(engine, g[:].rearrange("p (c i) j -> p c j i", i=4), raws[c][:].rearrange("p j (c i) -> p c j i", i=4))
            cols = slice(starts[c], starts[c] + size)
            nc.vector.quantize_mx(codes[:, cols].bitcast(FP8X4), planes[:, cols], g[:].rearrange("p w j -> p (w j)"))

        def weight(name):
            raw, bf, wc, ws, _ = wt[name]
            engines = W_ENGINES[name]
            if name == "w2":
                copy(engines[0], bf[:].rearrange("p (c i j) -> p c j i", i=4, j=PACK), raw[:].rearrange("p j (c i) -> p c j i", i=4))
                nc.vector.quantize_mx(wc[:].bitcast(FP8X4), ws[:], bf[:])
                return
            for u in range(2):
                half = slice(u * 1024, (u + 1) * 1024)
                copy(engines[u], bf[:, half].rearrange("p (t m j) -> p m t j", t=2, j=PACK),
                     raw[:].rearrange("p j (m t) -> p m t j", t=PACK)[:, :, 2 * u : 2 * u + 2, :])
            for u in range(2):
                half = slice(u * 1024, (u + 1) * 1024)
                cols = slice(u * 256, (u + 1) * 256)
                nc.vector.quantize_mx(wc[:, cols].bitcast(FP8X4), ws[:, cols], bf[:, half])

        def gather(s):
            a, b = SLICES[s]
            window = T - S + b
            words = keep.tile([P, b - a], U32, name="words%d" % s, align_bytes=64)
            scales = keep.tile([P, b - a], U8, name="scales%d" % s, align_bytes=64)
            picked[s] = (words, scales)
            places = offsets[:, a // 16 : b // 16]
            nc.vector.tensor_copy(words[:], codes[:, 0:window].indirect(places))
            nc.vector.tensor_copy(scales[:], planes[:, 0:window].indirect(places))

        def product(bank, name, s, j):
            words, scales = picked[s]
            wc, ws = wt[name][2], wt[name][3]
            for t in range(PACK):
                cols = slice(t * P, (t + 1) * P)
                nc.tensor.matmul_mx(
                    out=bank[:, cols],
                    lhsT=wc[:, cols].bitcast(FP8X4), lhsT_scale=ws[:, cols],
                    rhs=words[:, j : j + SUB].bitcast(FP8X4), rhs_scale=scales[:, j : j + SUB],
                    start=True, stop=True)

        def up(s):
            a, b = SLICES[s]
            for j in range(0, b - a, SUB):
                g = gates.tile([P, SUB, PACK], F32, name="g")
                gelus[s, j] = g
                bank = psum.tile([P, PACK, SUB], F32, name="bank1")
                product(bank[:].rearrange("p t n -> p (t n)"), "w1", s, j)
                nc.scalar.activation(g[:], bank[:].rearrange("p t n -> p n t"), GELU)

        def down(s):
            a, b = SLICES[s]
            j = 0
            while j < b - a:
                n = min(2 * SUB, b - a - j)
                h = hidden.tile([P, 2 * SUB, PACK], BF16, name="h", align_bytes=64)
                for q in range(0, n, SUB):
                    bank = psum.tile([P, PACK, SUB], F32, name="bank3")
                    product(bank[:].rearrange("p t n -> p (t n)"), "w3", s, j + q)
                    nc.vector.tensor_tensor(h[:, q : q + SUB, :], bank[:].rearrange("p t n -> p n t"), gelus[s, j + q][:], MULT)
                h_codes = hidden.tile([P, 2 * SUB], U32, name="h_codes", align_bytes=64)
                h_planes = hidden.tile([P, 2 * SUB], U8, name="h_planes", align_bytes=64)
                nc.vector.quantize_mx(h_codes[:, 0:n].bitcast(FP8X4), h_planes[:, 0:n], h[:, 0:n, :].rearrange("p n t -> p (n t)"))
                y = psum_y.tile([P, 2, 2 * SUB], F32, name="y")
                wc, ws = wt["w2"][2], wt["w2"][3]
                for m in range(N // P):
                    cols = slice(m * P, (m + 1) * P)
                    nc.tensor.matmul_mx(
                        out=y[:, m, 0:n],
                        lhsT=wc[:, cols].bitcast(FP8X4), lhsT_scale=ws[:, cols],
                        rhs=h_codes[:, 0:n].bitcast(FP8X4), rhs_scale=h_planes[:, 0:n],
                        start=True, stop=True)
                j0 = a + j
                view = out.rearrange("(m p) n -> p m n", p=P)[:, :, j0 : j0 + n]
                j += n
                if j0 + n == S:
                    for m in range(2):
                        y_half = hidden.tile([P, 2 * SUB], F32, name="y_half%d" % m)
                        copy("vs"[m], y_half[:, 0:n], y[:, m, 0:n])
                        nc.sync.dma_start(view[:, m, :], y_half[:, 0:n])
                else:
                    y_sb = hidden.tile([P, 2, 2 * SUB], F32, name="y_sb")
                    copy(Y_ENGINES[j0 // SUB], y_sb[:, :, 0:n], y[:, :, 0:n])
                    nc.sync.dma_start(view, y_sb[:, :, 0:n])

        for item in TEXT:
            if item[0] == "x":
                chunk(int(item[1:]))
            elif item[0] == "w":
                weight(item)
            elif item[0] == "g":
                gather(int(item[1:]))
            elif item[0] == "u":
                up(int(item[1:]))
            else:
                down(int(item[1:]))
